import numpy as np
import ml_dtypes


def mxq(x, axis, fmt="e4m3"):
    dtype, down = {"e4m3": (ml_dtypes.float8_e4m3fn, 7), "e5m2": (ml_dtypes.float8_e5m2, 14)}[fmt]
    v = np.moveaxis(np.asarray(x, np.float32).astype(ml_dtypes.bfloat16).astype(np.float64), axis, -1)
    blocks = v.reshape(v.shape[:-1] + (-1, 32))
    amax = np.abs(blocks).max(-1, keepdims=True)
    byte = np.maximum(np.where(amax > 0, np.frexp(amax)[1] - 1 + 127, 0) - down, 1)
    scale = np.exp2(byte - 127.0)
    codes = (blocks / scale).astype(np.float32).astype(dtype).astype(np.float64)
    return np.moveaxis((codes * scale).reshape(v.shape), -1, axis)


WIDE = False


def mx_kscale(k):
    if not WIDE:
        return np.ones(k)
    levels = np.array([10, -10, 5, -5, 0])
    if k % 512:
        return np.exp2(np.random.permutation(np.resize(levels, k // 32))).repeat(32)
    a = np.empty((k // 512, 16))
    for p in range(k // 512):
        a[p, :8] = np.random.permutation(np.resize(levels, 8))
        for g in range(8):
            far = levels[np.abs(levels - a[p, g]) >= 10]
            a[p, g + 8] = far[np.random.randint(len(far))]
    return np.exp2(a.ravel()).repeat(32)


def f64(x):
    return np.asarray(x).astype(np.float64)


def striped(idx):
    return np.tile(idx.reshape(-1, 16).T, (8, 1)).astype(np.uint16)


def unstriped(offs):
    return offs[:16].T.reshape(-1).astype(np.int64)


E2M1 = np.array([0.0, 0.5, 1.0, 1.5, 2.0, 3.0, 4.0, 6.0, -0.0, -0.5, -1.0, -1.5, -2.0, -3.0, -4.0, -6.0])


def pack_weight(w, fmt):
    k, n = w.shape
    w = f64(np.asarray(w, np.float32).astype(ml_dtypes.bfloat16)).reshape(k // 32, 32, n)
    amax = np.abs(w).max(1)
    if fmt == "e4m3":
        byte = np.frexp(amax)[1] - 1 + 127 - 7
    else:
        mant, ex = np.frexp(amax / 6.0)
        byte = np.where(mant > 0.5, ex, ex - 1) + 127
    byte = np.clip(np.where(amax > 0, byte, 1), 1, 254)
    scaled = (w * np.exp2(127.0 - byte)[:, None, :]).reshape(k, n).astype(np.float32)
    by_word = np.ascontiguousarray(scaled.reshape(k // 512, 128, 4, n).transpose(0, 1, 3, 2))
    if fmt == "e4m3":
        words = by_word.astype(ml_dtypes.float8_e4m3fn).view(np.uint8)
    else:
        c = by_word.astype(ml_dtypes.float4_e2m1fn).view(np.uint8) & 0xF
        words = (c[..., 0::2] | (c[..., 1::2] << 4)).reshape(k // 512, 128, 2 * n)
    return np.ascontiguousarray(words), np.ascontiguousarray(byte.astype(np.uint8).reshape(k // 512, 16, n))


def unpack_weight(words, scales, fmt):
    g, _, n = scales.shape
    words = np.ascontiguousarray(words).reshape(g, 128, n, -1)
    if fmt == "e4m3":
        vals = words.view(ml_dtypes.float8_e4m3fn).astype(np.float64)
    else:
        nib = np.empty((g, 128, n, 4), np.uint8)
        nib[..., 0::2] = words & 0xF
        nib[..., 1::2] = words >> 4
        vals = E2M1[nib]
    vals = vals * np.repeat(np.exp2(scales.astype(np.float64) - 127.0), 8, axis=1)[..., None]
    return vals.transpose(0, 1, 3, 2).reshape(g * 512, n)


def pack_table(v):
    words, scales = pack_weight(v, "e4m3")
    return np.concatenate([words.reshape(words.shape[0], -1), scales.reshape(scales.shape[0], -1)], axis=1)


def unpack_table(tab):
    g, t = tab.shape[0], tab.shape[1] // 528
    return unpack_weight(tab[:, :512 * t].reshape(g, 128, t, 4), tab[:, 512 * t:].reshape(g, 16, t), "e4m3")


K, L, M, T, S = 1536, 512, 128, 1024, 512


def setup_inputs():
    n = np.random.standard_normal
    s1 = mx_kscale(K)[:, None]
    s2 = mx_kscale(L)[:, None]
    p_w4 = pack_weight(n((K, M)) / np.sqrt(K) / s1, "e2m1")
    return {
        "tab": pack_table(n((K, T)) * s1),
        "w4_words": p_w4[0],
        "w4_scales": p_w4[1],
        "x": (n((L, S)) * s2).astype(np.float32),
        "u": (n((L, M)) / np.sqrt(L) / s2).astype(np.float32),
        "offs": striped(np.random.permutation(T)[:S]),
    }


def reference(tab, w4_words, w4_scales, x, u, offs):
    tab_ = unpack_table(tab)[:, unstriped(offs)]
    w4_ = unpack_weight(w4_words, w4_scales, "e2m1")
    x_ = mxq(f64(x), 0, "e4m3")
    u_ = mxq(f64(u), 0, "e4m3")
    y = tab_.T @ w4_ + x_.T @ u_
    return y

@@ -1,0 +1,138 @@
+import concourse.mybir as mybir
+
+K, L, M, T, S = 1536, 512, 128, 1024, 512
+FLOPS = 2 * S * M * (K + L)
+
+F32 = mybir.dt.float32
+BF16 = mybir.dt.bfloat16
+I32 = mybir.dt.int32
+U32 = mybir.dt.uint32
+U16 = mybir.dt.uint16
+U8 = mybir.dt.uint8
+E4M3 = mybir.dt.float8_e4m3fn_x4
+E2M1 = mybir.dt.float4_e2m1fn_x4
+
+P = 128
+PASSES = K // 512
+HALF = S // 2
+TILES = S // P
+
+
+def tile_list_tabx_tm_none_kernel(tc, tab, w4_words, w4_scales, x, u, offs, out):
+    nc = tc.nc
+    with (
+        tc.tile_pool(name="keep", bufs=1) as keep,
+        tc.psum_pool(name="psum", bufs=1) as psum,
+    ):
+        offsets = keep.tile([P, S // 16], U16, name="offsets")
+        nc.sync.dma_start(offsets[:], offs)
+
+        tab_scales = keep.tile([P, PASSES, T // 4], I32, name="tab_scales", align_bytes=64)
+        nc.vector.memset(tab_scales[:], 0)
+        scale_rows = tab[:, 512 * T :].rearrange("a (q t) -> q a t", t=T)
+        for quad in range(4):
+            nc.sync.dma_start(
+                tab_scales[32 * quad : 32 * quad + 4, :, :],
+                scale_rows[4 * quad : 4 * quad + 4, :, :].bitcast(I32),
+            )
+
+        u_raw = keep.tile([P, 4, M], F32, name="u_raw")
+        nc.sync.dma_start(u_raw[:], u.rearrange("(p j) n -> p j n", j=4))
+        x_raw = []
+        x_rows = x.rearrange("(p j) s -> p j s", j=4)
+        for h in range(2):
+            raw = keep.tile([P, 4, HALF], F32, name="x_raw%d" % h)
+            nc.sync.dma_start(raw[:], x_rows[:, :, h * HALF : (h + 1) * HALF])
+            x_raw.append(raw)
+        tab_words = []
+        for a in range(PASSES):
+            words = keep.tile([P, T], I32, name="tab_words%d" % a, align_bytes=64)
+            nc.sync.dma_start(words[:], tab[a, 0 : 512 * T].rearrange("(p c) -> p c", p=P).bitcast(I32))
+            tab_words.append(words)
+
+        w_codes = keep.tile([P, PASSES, 2 * M], U8, name="w_codes", align_bytes=64)
+        w_scales = keep.tile([P, PASSES, M], U8, name="w_scales", align_bytes=64)
+        warm = keep.tile([P, 1], F32, name="warm")
+        warmed = keep.tile([P, 1], F32, name="warmed")
+        nc.gpsimd.memset(warm[:], 0.0)
+        nc.scalar.copy(warmed[:], warm[:])
+        nc.gpsimd.memset(w_scales[:].bitcast(I32), 0)
+        nc.gpsimd.dma_start(w_codes[:].bitcast(I32), w4_words.rearrange("a p c -> p a c").bitcast(I32))
+        w_scale_rows = w4_scales.rearrange("a q n -> q a n")
+        for quad in range(4):
+            nc.gpsimd.dma_start(
+                w_scales[32 * quad : 32 * quad + 4, :, :].bitcast(I32),
+                w_scale_rows[4 * quad : 4 * quad + 4, :, :].bitcast(I32),
+            )
+
+        u_bf = keep.tile([P, M, 4], BF16, name="u_bf", align_bytes=64)
+        nc.scalar.copy(u_bf[:], u_raw[:].rearrange("p j n -> p n j"))
+        x_bf = []
+        for h in range(2):
+            bf = keep.tile([P, HALF, 4], BF16, name="x_bf%d" % h, align_bytes=64)
+            nc.scalar.copy(bf[:], x_raw[h][:].rearrange("p j s -> p s j"))
+            x_bf.append(bf)
+
+        picked_scales = []
+        for a in range(PASSES):
+            picked = keep.tile([P, S], U8, name="picked_scales%d" % a, align_bytes=64)
+            nc.vector.tensor_copy(picked[:], tab_scales[:, a, :].bitcast(U8).indirect(offsets[:]))
+            picked_scales.append(picked)
+
+        u_codes = keep.tile([P, M], U32, name="u_codes", align_bytes=64)
+        u_scales = keep.tile([P, M], U8, name="u_scales", align_bytes=64)
+        x_codes = keep.tile([P, S], U32, name="x_codes", align_bytes=64)
+        x_scales = keep.tile([P, S], U8, name="x_scales", align_bytes=64)
+        nc.vector.quantize_mx(u_codes[:].bitcast(E4M3), u_scales[:], u_bf[:].rearrange("p n j -> p (n j)"))
+
+        picked_words = [
+            keep.tile([P, S], U32, name="picked_words%d" % a, align_bytes=64) for a in range(PASSES)
+        ]
+        acc = [psum.tile([P, M], F32, name="acc%d" % c) for c in range(TILES)]
+
+        def gather_words(a, c0, c1):
+            nc.vector.tensor_copy(
+                picked_words[a][:, c0:c1],
+                tab_words[a][:].bitcast(U32).indirect(offsets[:, c0 // 16 : c1 // 16]),
+            )
+
+        def table_pass(a, c):
+            cols = slice(c * P, (c + 1) * P)
+            nc.tensor.matmul_mx(
+                out=acc[c][:],
+                lhsT=picked_words[a][:, cols].bitcast(E4M3),
+                lhsT_scale=picked_scales[a][:, cols],
+                rhs=w_codes[:, a, :].bitcast(E2M1),
+                rhs_scale=w_scales[:, a, :],
+                start=False,
+                stop=(a == PASSES - 1),
+            )
+
+        gather_words(0, 0, S)
+        for h in range(2):
+            cols = slice(h * HALF, (h + 1) * HALF)
+            nc.vector.quantize_mx(
+                x_codes[:, cols].bitcast(E4M3), x_scales[:, cols], x_bf[h][:].rearrange("p s j -> p (s j)")
+            )
+        gather_words(1, 0, S)
+
+        for c in range(TILES):
+            cols = slice(c * P, (c + 1) * P)
+            nc.tensor.matmul_mx(
+                out=acc[c][:],
+                lhsT=x_codes[:, cols].bitcast(E4M3),
+                lhsT_scale=x_scales[:, cols],
+                rhs=u_codes[:].bitcast(E4M3),
+                rhs_scale=u_scales[:],
+                start=True,
+                stop=False,
+            )
+        for a in range(PASSES - 1):
+            for c in range(TILES):
+                table_pass(a, c)
+        for c in range(TILES):
+            gather_words(PASSES - 1, c * P, (c + 1) * P)
+            table_pass(PASSES - 1, c)
+            result = keep.tile([P, M], F32, name="result%d" % c)
+            nc.scalar.copy(result[:], acc[c][:])
+            nc.sync.dma_start(out[c * P : (c + 1) * P, :], result[:])

@@ -27,43 +27,58 @@ def tile_list_tabx_tm_none_kernel(tc, tab, w4_words, w4_scales, x, u, offs, out)
         offsets = keep.tile([P, S // 16], U16, name="offsets")
         nc.sync.dma_start(offsets[:], offs)
 
-        tab_scales = keep.tile([P, PASSES, T // 4], I32, name="tab_scales", align_bytes=64)
-        nc.vector.memset(tab_scales[:], 0)
-        scale_rows = tab[:, 512 * T :].rearrange("a (q t) -> q a t", t=T)
+        scales01 = keep.tile([P, T // 4], I32, name="scales01", align_bytes=64)
+        nc.vector.memset(scales01[:], 0)
+        scale_rows = tab[:, 512 * T :].rearrange("a (q t) -> a q t", t=T)
         for quad in range(4):
             nc.sync.dma_start(
-                tab_scales[32 * quad : 32 * quad + 4, :, :],
-                scale_rows[4 * quad : 4 * quad + 4, :, :].bitcast(I32),
+                scales01[32 * quad : 32 * quad + 8, :],
+                scale_rows[0:2, 4 * quad : 4 * quad + 4, :].bitcast(I32),
             )
 
-        u_raw = keep.tile([P, 4, M], F32, name="u_raw")
-        nc.sync.dma_start(u_raw[:], u.rearrange("(p j) n -> p j n", j=4))
-        x_raw = []
-        x_rows = x.rearrange("(p j) s -> p j s", j=4)
-        for h in range(2):
-            raw = keep.tile([P, 4, HALF], F32, name="x_raw%d" % h)
-            nc.sync.dma_start(raw[:], x_rows[:, :, h * HALF : (h + 1) * HALF])
-            x_raw.append(raw)
-        tab_words = []
-        for a in range(PASSES):
+        def load_words(a):
             words = keep.tile([P, T], I32, name="tab_words%d" % a, align_bytes=64)
             nc.sync.dma_start(words[:], tab[a, 0 : 512 * T].rearrange("(p c) -> p c", p=P).bitcast(I32))
-            tab_words.append(words)
+            return words
 
+        x_rows = x.rearrange("(p j) s -> p j s", j=4)
+
+        def load_x(h):
+            raw = keep.tile([P, 4, HALF], F32, name="x_raw%d" % h)
+            nc.sync.dma_start(raw[:], x_rows[:, :, h * HALF : (h + 1) * HALF])
+            return raw
+
+        tab_words = [load_words(0)]
+        u_raw = keep.tile([P, 4, M], F32, name="u_raw")
+        nc.sync.dma_start(u_raw[:], u.rearrange("(p j) n -> p j n", j=4))
+        x_raw = [load_x(0)]
+        scales2 = keep.tile([P, T // 4], I32, name="scales2", align_bytes=64)
+        nc.vector.memset(scales2[:], 0)
+        for quad in range(4):
+            nc.sync.dma_start(
+                scales2[32 * quad : 32 * quad + 4, :],
+                scale_rows[2, 4 * quad : 4 * quad + 4, :].bitcast(I32),
+            )
+        x_raw.append(load_x(1))
         w_codes = keep.tile([P, PASSES, 2 * M], U8, name="w_codes", align_bytes=64)
+        nc.sync.dma_start(w_codes[:].bitcast(I32), w4_words.rearrange("a p c -> p a c").bitcast(I32))
+        tab_words.append(load_words(1))
+        tab_words.append(load_words(2))
+
         w_scales = keep.tile([P, PASSES, M], U8, name="w_scales", align_bytes=64)
-        warm = keep.tile([P, 1], F32, name="warm")
-        warmed = keep.tile([P, 1], F32, name="warmed")
-        nc.gpsimd.memset(warm[:], 0.0)
-        nc.scalar.copy(warmed[:], warm[:])
         nc.gpsimd.memset(w_scales[:].bitcast(I32), 0)
-        nc.gpsimd.dma_start(w_codes[:].bitcast(I32), w4_words.rearrange("a p c -> p a c").bitcast(I32))
         w_scale_rows = w4_scales.rearrange("a q n -> q a n")
         for quad in range(4):
             nc.gpsimd.dma_start(
                 w_scales[32 * quad : 32 * quad + 4, :, :].bitcast(I32),
                 w_scale_rows[4 * quad : 4 * quad + 4, :, :].bitcast(I32),
             )
+        warm = keep.tile([P, 1], F32, name="warm")
+        warmed = keep.tile([P, 1], F32, name="warmed")
+        nc.vector.memset(warm[:], 0.0)
+        nc.scalar.copy(warmed[:], warm[:])
+        picked1 = keep.tile([P, S], U8, name="picked1", align_bytes=64)
+        nc.vector.memset(picked1[:].bitcast(I32), 0)
 
         u_bf = keep.tile([P, M, 4], BF16, name="u_bf", align_bytes=64)
         nc.scalar.copy(u_bf[:], u_raw[:].rearrange("p j n -> p n j"))
@@ -73,17 +88,18 @@ def tile_list_tabx_tm_none_kernel(tc, tab, w4_words, w4_scales, x, u, offs, out)
             nc.scalar.copy(bf[:], x_raw[h][:].rearrange("p j s -> p s j"))
             x_bf.append(bf)
 
-        picked_scales = []
-        for a in range(PASSES):
-            picked = keep.tile([P, S], U8, name="picked_scales%d" % a, align_bytes=64)
-            nc.vector.tensor_copy(picked[:], tab_scales[:, a, :].bitcast(U8).indirect(offsets[:]))
-            picked_scales.append(picked)
+        picked01 = keep.tile([P, S], U8, name="picked01", align_bytes=64)
+        nc.vector.tensor_copy(picked01[:], scales01[:].bitcast(U8).indirect(offsets[:]))
+        for quad in range(4):
+            nc.sync.dma_start(
+                picked1[32 * quad : 32 * quad + 4, :].bitcast(I32),
+                picked01[32 * quad + 4 : 32 * quad + 8, :].bitcast(I32),
+            )
 
         u_codes = keep.tile([P, M], U32, name="u_codes", align_bytes=64)
         u_scales = keep.tile([P, M], U8, name="u_scales", align_bytes=64)
         x_codes = keep.tile([P, S], U32, name="x_codes", align_bytes=64)
         x_scales = keep.tile([P, S], U8, name="x_scales", align_bytes=64)
-        nc.vector.quantize_mx(u_codes[:].bitcast(E4M3), u_scales[:], u_bf[:].rearrange("p n j -> p (n j)"))
 
         picked_words = [
             keep.tile([P, S], U32, name="picked_words%d" % a, align_bytes=64) for a in range(PASSES)
@@ -109,6 +125,10 @@ def tile_list_tabx_tm_none_kernel(tc, tab, w4_words, w4_scales, x, u, offs, out)
             )
 
         gather_words(0, 0, S)
+        picked2 = keep.tile([P, S], U8, name="picked2", align_bytes=64)
+        nc.vector.tensor_copy(picked2[:], scales2[:].bitcast(U8).indirect(offsets[:]))
+        picked_scales = [picked01, picked1, picked2]
+        nc.vector.quantize_mx(u_codes[:].bitcast(E4M3), u_scales[:], u_bf[:].rearrange("p n j -> p (n j)"))
         for h in range(2):
             cols = slice(h * HALF, (h + 1) * HALF)
             nc.vector.quantize_mx(

@@ -28,10 +28,20 @@ def tile_list_tabx_tm_none_kernel(tc, tab, w4_words, w4_scales, x, u, offs, out)
         nc.sync.dma_start(offsets[:], offs)
 
         scales01 = keep.tile([P, T // 4], I32, name="scales01", align_bytes=64)
-        nc.vector.memset(scales01[:], 0)
+        nc.gpsimd.memset(scales01[:], 0)
+        w_scales = keep.tile([P, PASSES, M], U8, name="w_scales", align_bytes=64)
+        nc.gpsimd.memset(w_scales[:].bitcast(I32), 0)
+        scales2 = keep.tile([P, T // 4], I32, name="scales2", align_bytes=64)
+        nc.vector.memset(scales2[:], 0)
+        picked1 = keep.tile([P, S], U8, name="picked1", align_bytes=64)
+        nc.vector.memset(picked1[:].bitcast(I32), 0)
+        warm = keep.tile([P, 1], F32, name="warm")
+        warmed = keep.tile([P, 1], F32, name="warmed")
+        nc.vector.memset(warm[:], 0.0)
+
         scale_rows = tab[:, 512 * T :].rearrange("a (q t) -> a q t", t=T)
-        for quad in range(4):
-            nc.sync.dma_start(
+        for quad, queue in enumerate((nc.sync, nc.scalar, nc.sync, nc.scalar)):
+            queue.dma_start(
                 scales01[32 * quad : 32 * quad + 8, :],
                 scale_rows[0:2, 4 * quad : 4 * quad + 4, :].bitcast(I32),
             )
@@ -51,9 +61,14 @@ def tile_list_tabx_tm_none_kernel(tc, tab, w4_words, w4_scales, x, u, offs, out)
         tab_words = [load_words(0)]
         u_raw = keep.tile([P, 4, M], F32, name="u_raw")
         nc.sync.dma_start(u_raw[:], u.rearrange("(p j) n -> p j n", j=4))
+        w_scale_rows = w4_scales.rearrange("a q n -> q a n")
+        for quad in range(4):
+            nc.scalar.dma_start(
+                w_scales[32 * quad : 32 * quad + 4, :, :].bitcast(I32),
+                w_scale_rows[4 * quad : 4 * quad + 4, :, :].bitcast(I32),
+            )
+        nc.scalar.copy(warmed[:], warm[:])
         x_raw = [load_x(0)]
-        scales2 = keep.tile([P, T // 4], I32, name="scales2", align_bytes=64)
-        nc.vector.memset(scales2[:], 0)
         for quad in range(4):
             nc.sync.dma_start(
                 scales2[32 * quad : 32 * quad + 4, :],
@@ -64,21 +79,6 @@ def tile_list_tabx_tm_none_kernel(tc, tab, w4_words, w4_scales, x, u, offs, out)
         nc.sync.dma_start(w_codes[:].bitcast(I32), w4_words.rearrange("a p c -> p a c").bitcast(I32))
         tab_words.append(load_words(1))
         tab_words.append(load_words(2))
-
-        w_scales = keep.tile([P, PASSES, M], U8, name="w_scales", align_bytes=64)
-        nc.gpsimd.memset(w_scales[:].bitcast(I32), 0)
-        w_scale_rows = w4_scales.rearrange("a q n -> q a n")
-        for quad in range(4):
-            nc.gpsimd.dma_start(
-                w_scales[32 * quad : 32 * quad + 4, :, :].bitcast(I32),
-                w_scale_rows[4 * quad : 4 * quad + 4, :, :].bitcast(I32),
-            )
-        warm = keep.tile([P, 1], F32, name="warm")
-        warmed = keep.tile([P, 1], F32, name="warmed")
-        nc.vector.memset(warm[:], 0.0)
-        nc.scalar.copy(warmed[:], warm[:])
-        picked1 = keep.tile([P, S], U8, name="picked1", align_bytes=64)
-        nc.vector.memset(picked1[:].bitcast(I32), 0)
 
         u_bf = keep.tile([P, M, 4], BF16, name="u_bf", align_bytes=64)
         nc.scalar.copy(u_bf[:], u_raw[:].rearrange("p j n -> p n j"))
@@ -120,7 +120,7 @@ def tile_list_tabx_tm_none_kernel(tc, tab, w4_words, w4_scales, x, u, offs, out)
                 lhsT_scale=picked_scales[a][:, cols],
                 rhs=w_codes[:, a, :].bitcast(E2M1),
                 rhs_scale=w_scales[:, a, :],
-                start=False,
+                start=(a == 0),
                 stop=(a == PASSES - 1),
             )
 
@@ -129,14 +129,14 @@ def tile_list_tabx_tm_none_kernel(tc, tab, w4_words, w4_scales, x, u, offs, out)
         nc.vector.tensor_copy(picked2[:], scales2[:].bitcast(U8).indirect(offsets[:]))
         picked_scales = [picked01, picked1, picked2]
         nc.vector.quantize_mx(u_codes[:].bitcast(E4M3), u_scales[:], u_bf[:].rearrange("p n j -> p (n j)"))
-        for h in range(2):
+
+        def quantize_x(h):
             cols = slice(h * HALF, (h + 1) * HALF)
             nc.vector.quantize_mx(
                 x_codes[:, cols].bitcast(E4M3), x_scales[:, cols], x_bf[h][:].rearrange("p s j -> p (s j)")
             )
-        gather_words(1, 0, S)
 
-        for c in range(TILES):
+        def dense_pass(c):
             cols = slice(c * P, (c + 1) * P)
             nc.tensor.matmul_mx(
                 out=acc[c][:],
@@ -144,12 +144,21 @@ def tile_list_tabx_tm_none_kernel(tc, tab, w4_words, w4_scales, x, u, offs, out)
                 lhsT_scale=x_scales[:, cols],
                 rhs=u_codes[:].bitcast(E4M3),
                 rhs_scale=u_scales[:],
-                start=True,
+                start=False,
                 stop=False,
             )
-        for a in range(PASSES - 1):
-            for c in range(TILES):
-                table_pass(a, c)
+
+        for c in range(TILES):
+            table_pass(0, c)
+        quantize_x(0)
+        for c in range(TILES // 2):
+            dense_pass(c)
+        gather_words(1, 0, S)
+        for c in range(TILES):
+            table_pass(1, c)
+        quantize_x(1)
+        for c in range(TILES // 2, TILES):
+            dense_pass(c)
         for c in range(TILES):
             gather_words(PASSES - 1, c * P, (c + 1) * P)
             table_pass(PASSES - 1, c)

@@ -29,22 +29,15 @@ def tile_list_tabx_tm_none_kernel(tc, tab, w4_words, w4_scales, x, u, offs, out)
 
         scales01 = keep.tile([P, T // 4], I32, name="scales01", align_bytes=64)
         nc.gpsimd.memset(scales01[:], 0)
+        scales2 = keep.tile([P, T // 4], I32, name="scales2", align_bytes=64)
         w_scales = keep.tile([P, PASSES, M], U8, name="w_scales", align_bytes=64)
         nc.gpsimd.memset(w_scales[:].bitcast(I32), 0)
-        scales2 = keep.tile([P, T // 4], I32, name="scales2", align_bytes=64)
-        nc.vector.memset(scales2[:], 0)
-        picked1 = keep.tile([P, S], U8, name="picked1", align_bytes=64)
-        nc.vector.memset(picked1[:].bitcast(I32), 0)
         warm = keep.tile([P, 1], F32, name="warm")
         warmed = keep.tile([P, 1], F32, name="warmed")
         nc.vector.memset(warm[:], 0.0)
-
-        scale_rows = tab[:, 512 * T :].rearrange("a (q t) -> a q t", t=T)
-        for quad, queue in enumerate((nc.sync, nc.scalar, nc.sync, nc.scalar)):
-            queue.dma_start(
-                scales01[32 * quad : 32 * quad + 8, :],
-                scale_rows[0:2, 4 * quad : 4 * quad + 4, :].bitcast(I32),
-            )
+        picked = [keep.tile([P, S], U8, name="picked%d" % a, align_bytes=64) for a in range(PASSES)]
+        nc.vector.memset(scales2[:], 0)
+        nc.vector.memset(picked[1][:].bitcast(I32), 0)
 
         def load_words(a):
             words = keep.tile([P, T], I32, name="tab_words%d" % a, align_bytes=64)
@@ -58,49 +51,45 @@ def tile_list_tabx_tm_none_kernel(tc, tab, w4_words, w4_scales, x, u, offs, out)
             nc.sync.dma_start(raw[:], x_rows[:, :, h * HALF : (h + 1) * HALF])
             return raw
 
-        tab_words = [load_words(0)]
-        u_raw = keep.tile([P, 4, M], F32, name="u_raw")
-        nc.sync.dma_start(u_raw[:], u.rearrange("(p j) n -> p j n", j=4))
-        w_scale_rows = w4_scales.rearrange("a q n -> q a n")
-        for quad in range(4):
-            nc.scalar.dma_start(
-                w_scales[32 * quad : 32 * quad + 4, :, :].bitcast(I32),
-                w_scale_rows[4 * quad : 4 * quad + 4, :, :].bitcast(I32),
-            )
-        nc.scalar.copy(warmed[:], warm[:])
-        x_raw = [load_x(0)]
+        scale_rows = tab[:, 512 * T :].rearrange("a (q t) -> a q t", t=T)
         for quad in range(4):
             nc.sync.dma_start(
+                scales01[32 * quad : 32 * quad + 8, :],
+                scale_rows[0:2, 4 * quad : 4 * quad + 4, :].bitcast(I32),
+            )
+        nc.scalar.copy(warmed[:], warm[:])
+        tab_words = [load_words(0)]
+        x_raw = [load_x(0)]
+        u_raw = keep.tile([P, 4, M], F32, name="u_raw")
+        nc.sync.dma_start(u_raw[:], u.rearrange("(p j) n -> p j n", j=4))
+        for quad in range(4):
+            nc.scalar.dma_start(
                 scales2[32 * quad : 32 * quad + 4, :],
                 scale_rows[2, 4 * quad : 4 * quad + 4, :].bitcast(I32),
             )
-        x_raw.append(load_x(1))
-        w_codes = keep.tile([P, PASSES, 2 * M], U8, name="w_codes", align_bytes=64)
-        nc.sync.dma_start(w_codes[:].bitcast(I32), w4_words.rearrange("a p c -> p a c").bitcast(I32))
         tab_words.append(load_words(1))
         tab_words.append(load_words(2))
-
-        u_bf = keep.tile([P, M, 4], BF16, name="u_bf", align_bytes=64)
-        nc.scalar.copy(u_bf[:], u_raw[:].rearrange("p j n -> p n j"))
-        x_bf = []
-        for h in range(2):
-            bf = keep.tile([P, HALF, 4], BF16, name="x_bf%d" % h, align_bytes=64)
-            nc.scalar.copy(bf[:], x_raw[h][:].rearrange("p j s -> p s j"))
-            x_bf.append(bf)
-
-        picked01 = keep.tile([P, S], U8, name="picked01", align_bytes=64)
-        nc.vector.tensor_copy(picked01[:], scales01[:].bitcast(U8).indirect(offsets[:]))
-        for quad in range(4):
-            nc.sync.dma_start(
-                picked1[32 * quad : 32 * quad + 4, :].bitcast(I32),
-                picked01[32 * quad + 4 : 32 * quad + 8, :].bitcast(I32),
+        w_codes = keep.tile([P, PASSES, 2 * M], U8, name="w_codes", align_bytes=64)
+        nc.sync.dma_start(w_codes[:].bitcast(I32), w4_words.rearrange("a p c -> p a c").bitcast(I32))
+        w_scale_rows = w4_scales.rearrange("a q n -> q a n")
+        for quad, queue in enumerate((nc.gpsimd, nc.gpsimd, nc.sync, nc.sync)):
+            queue.dma_start(
+                w_scales[32 * quad : 32 * quad + 4, :, :].bitcast(I32),
+                w_scale_rows[4 * quad : 4 * quad + 4, :, :].bitcast(I32),
             )
+        x_raw.append(load_x(1))
+
+        x_bf = [keep.tile([P, HALF, 4], BF16, name="x_bf0", align_bytes=64)]
+        u_bf = keep.tile([P, M, 4], BF16, name="u_bf", align_bytes=64)
+        nc.scalar.copy(x_bf[0][:], x_raw[0][:].rearrange("p j s -> p s j"))
+        nc.scalar.copy(u_bf[:], u_raw[:].rearrange("p j n -> p n j"))
+        x_bf += [keep.tile([P, P, 4], BF16, name="x_bf%d" % h, align_bytes=64) for h in range(1, 3)]
+        nc.scalar.copy(x_bf[1][:], x_raw[1][:, :, 0:P].rearrange("p j s -> p s j"))
 
         u_codes = keep.tile([P, M], U32, name="u_codes", align_bytes=64)
         u_scales = keep.tile([P, M], U8, name="u_scales", align_bytes=64)
         x_codes = keep.tile([P, S], U32, name="x_codes", align_bytes=64)
         x_scales = keep.tile([P, S], U8, name="x_scales", align_bytes=64)
-
         picked_words = [
             keep.tile([P, S], U32, name="picked_words%d" % a, align_bytes=64) for a in range(PASSES)
         ]
@@ -112,28 +101,10 @@ def tile_list_tabx_tm_none_kernel(tc, tab, w4_words, w4_scales, x, u, offs, out)
                 tab_words[a][:].bitcast(U32).indirect(offsets[:, c0 // 16 : c1 // 16]),
             )
 
-        def table_pass(a, c):
-            cols = slice(c * P, (c + 1) * P)
-            nc.tensor.matmul_mx(
-                out=acc[c][:],
-                lhsT=picked_words[a][:, cols].bitcast(E4M3),
-                lhsT_scale=picked_scales[a][:, cols],
-                rhs=w_codes[:, a, :].bitcast(E2M1),
-                rhs_scale=w_scales[:, a, :],
-                start=(a == 0),
-                stop=(a == PASSES - 1),
-            )
-
-        gather_words(0, 0, S)
-        picked2 = keep.tile([P, S], U8, name="picked2", align_bytes=64)
-        nc.vector.tensor_copy(picked2[:], scales2[:].bitcast(U8).indirect(offsets[:]))
-        picked_scales = [picked01, picked1, picked2]
-        nc.vector.quantize_mx(u_codes[:].bitcast(E4M3), u_scales[:], u_bf[:].rearrange("p n j -> p (n j)"))
-
-        def quantize_x(h):
-            cols = slice(h * HALF, (h + 1) * HALF)
+        def quantize_x(bf, c0, c1):
+            cols = slice(c0, c1)
             nc.vector.quantize_mx(
-                x_codes[:, cols].bitcast(E4M3), x_scales[:, cols], x_bf[h][:].rearrange("p s j -> p (s j)")
+                x_codes[:, cols].bitcast(E4M3), x_scales[:, cols], bf[:].rearrange("p s j -> p (s j)")
             )
 
         def dense_pass(c):
@@ -145,23 +116,53 @@ def tile_list_tabx_tm_none_kernel(tc, tab, w4_words, w4_scales, x, u, offs, out)
                 rhs=u_codes[:].bitcast(E4M3),
                 rhs_scale=u_scales[:],
                 start=False,
-                stop=False,
+                stop=(c >= TILES // 2),
             )
 
-        for c in range(TILES):
-            table_pass(0, c)
-        quantize_x(0)
-        for c in range(TILES // 2):
-            dense_pass(c)
+        def table_pass(a, c):
+            cols = slice(c * P, (c + 1) * P)
+            nc.tensor.matmul_mx(
+                out=acc[c][:],
+                lhsT=picked_words[a][:, cols].bitcast(E4M3),
+                lhsT_scale=picked[a][:, cols],
+                rhs=w_codes[:, a, :].bitcast(E2M1),
+                rhs_scale=w_scales[:, a, :],
+                start=(a == 0),
+                stop=(a == PASSES - 1 and c < TILES // 2),
+            )
+
+        nc.vector.tensor_copy(picked[0][:], scales01[:].bitcast(U8).indirect(offsets[:]))
+        gather_words(0, 0, S)
+        for quad in range(4):
+            nc.sync.dma_start(
+                picked[1][32 * quad : 32 * quad + 4, :].bitcast(I32),
+                picked[0][32 * quad + 4 : 32 * quad + 8, :].bitcast(I32),
+            )
+        nc.vector.tensor_copy(picked[2][:], scales2[:].bitcast(U8).indirect(offsets[:]))
         gather_words(1, 0, S)
         for c in range(TILES):
-            table_pass(1, c)
-        quantize_x(1)
-        for c in range(TILES // 2, TILES):
+            table_pass(0, c)
+        quantize_x(x_bf[0], 0, HALF)
+        nc.vector.quantize_mx(u_codes[:].bitcast(E4M3), u_scales[:], u_bf[:].rearrange("p n j -> p (n j)"))
+        for c in range(TILES // 2):
             dense_pass(c)
         for c in range(TILES):
-            gather_words(PASSES - 1, c * P, (c + 1) * P)
-            table_pass(PASSES - 1, c)
+            table_pass(1, c)
+
+        def finish(c, copy):
             result = keep.tile([P, M], F32, name="result%d" % c)
-            nc.scalar.copy(result[:], acc[c][:])
+            copy(result[:], acc[c][:])
             nc.sync.dma_start(out[c * P : (c + 1) * P, :], result[:])
+
+        gather_words(PASSES - 1, 0, HALF)
+        for c in range(TILES // 2):
+            table_pass(PASSES - 1, c)
+            finish(c, nc.scalar.copy)
+        gather_words(PASSES - 1, HALF, S)
+        for c in range(TILES // 2, TILES):
+            table_pass(PASSES - 1, c)
+        nc.vector.tensor_copy(x_bf[2][:], x_raw[1][:, :, P:HALF].rearrange("p j s -> p s j"))
+        for c, copy in ((2, nc.scalar.copy), (3, nc.vector.tensor_copy)):
+            quantize_x(x_bf[c - 1], c * P, (c + 1) * P)
+            dense_pass(c)
+            finish(c, copy)

import concourse.mybir as mybir

K, L, M, T, S = 1536, 512, 128, 1024, 512
FLOPS = 2 * S * M * (K + L)

F32 = mybir.dt.float32
BF16 = mybir.dt.bfloat16
I32 = mybir.dt.int32
U32 = mybir.dt.uint32
U16 = mybir.dt.uint16
U8 = mybir.dt.uint8
E4M3 = mybir.dt.float8_e4m3fn_x4
E2M1 = mybir.dt.float4_e2m1fn_x4

P = 128
PASSES = K // 512
HALF = S // 2
TILES = S // P


def tile_list_tabx_tm_none_kernel(tc, tab, w4_words, w4_scales, x, u, offs, out):
    nc = tc.nc
    with (
        tc.tile_pool(name="keep", bufs=1) as keep,
        tc.psum_pool(name="psum", bufs=1) as psum,
    ):
        offsets = keep.tile([P, S // 16], U16, name="offsets")
        nc.sync.dma_start(offsets[:], offs)

        scales01 = keep.tile([P, T // 4], I32, name="scales01", align_bytes=64)
        nc.gpsimd.memset(scales01[:], 0)
        scales2 = keep.tile([P, T // 4], I32, name="scales2", align_bytes=64)
        w_scales = keep.tile([P, PASSES, M], U8, name="w_scales", align_bytes=64)
        nc.gpsimd.memset(w_scales[:].bitcast(I32), 0)
        warm = keep.tile([P, 1], F32, name="warm")
        warmed = keep.tile([P, 1], F32, name="warmed")
        nc.vector.memset(warm[:], 0.0)
        picked = [keep.tile([P, S], U8, name="picked%d" % a, align_bytes=64) for a in range(PASSES)]
        nc.vector.memset(scales2[:], 0)
        nc.vector.memset(picked[1][:].bitcast(I32), 0)

        def load_words(a):
            words = keep.tile([P, T], I32, name="tab_words%d" % a, align_bytes=64)
            nc.sync.dma_start(words[:], tab[a, 0 : 512 * T].rearrange("(p c) -> p c", p=P).bitcast(I32))
            return words

        x_rows = x.rearrange("(p j) s -> p j s", j=4)

        def load_x(h):
            raw = keep.tile([P, 4, HALF], F32, name="x_raw%d" % h)
            nc.sync.dma_start(raw[:], x_rows[:, :, h * HALF : (h + 1) * HALF])
            return raw

        scale_rows = tab[:, 512 * T :].rearrange("a (q t) -> a q t", t=T)
        for quad in range(4):
            nc.sync.dma_start(
                scales01[32 * quad : 32 * quad + 8, :],
                scale_rows[0:2, 4 * quad : 4 * quad + 4, :].bitcast(I32),
            )
        nc.scalar.copy(warmed[:], warm[:])
        tab_words = [load_words(0)]
        x_raw = [load_x(0)]
        u_raw = keep.tile([P, 4, M], F32, name="u_raw")
        nc.sync.dma_start(u_raw[:], u.rearrange("(p j) n -> p j n", j=4))
        for quad in range(4):
            nc.scalar.dma_start(
                scales2[32 * quad : 32 * quad + 4, :],
                scale_rows[2, 4 * quad : 4 * quad + 4, :].bitcast(I32),
            )
        tab_words.append(load_words(1))
        tab_words.append(load_words(2))
        w_codes = keep.tile([P, PASSES, 2 * M], U8, name="w_codes", align_bytes=64)
        nc.sync.dma_start(w_codes[:].bitcast(I32), w4_words.rearrange("a p c -> p a c").bitcast(I32))
        w_scale_rows = w4_scales.rearrange("a q n -> q a n")
        for quad, queue in enumerate((nc.gpsimd, nc.gpsimd, nc.sync, nc.sync)):
            queue.dma_start(
                w_scales[32 * quad : 32 * quad + 4, :, :].bitcast(I32),
                w_scale_rows[4 * quad : 4 * quad + 4, :, :].bitcast(I32),
            )
        x_raw.append(load_x(1))

        x_bf = [keep.tile([P, HALF, 4], BF16, name="x_bf0", align_bytes=64)]
        u_bf = keep.tile([P, M, 4], BF16, name="u_bf", align_bytes=64)
        nc.scalar.copy(x_bf[0][:], x_raw[0][:].rearrange("p j s -> p s j"))
        nc.scalar.copy(u_bf[:], u_raw[:].rearrange("p j n -> p n j"))
        x_bf += [keep.tile([P, P, 4], BF16, name="x_bf%d" % h, align_bytes=64) for h in range(1, 3)]
        nc.scalar.copy(x_bf[1][:], x_raw[1][:, :, 0:P].rearrange("p j s -> p s j"))

        u_codes = keep.tile([P, M], U32, name="u_codes", align_bytes=64)
        u_scales = keep.tile([P, M], U8, name="u_scales", align_bytes=64)
        x_codes = keep.tile([P, S], U32, name="x_codes", align_bytes=64)
        x_scales = keep.tile([P, S], U8, name="x_scales", align_bytes=64)
        picked_words = [
            keep.tile([P, S], U32, name="picked_words%d" % a, align_bytes=64) for a in range(PASSES)
        ]
        acc = [psum.tile([P, M], F32, name="acc%d" % c) for c in range(TILES)]

        def gather_words(a, c0, c1):
            nc.vector.tensor_copy(
                picked_words[a][:, c0:c1],
                tab_words[a][:].bitcast(U32).indirect(offsets[:, c0 // 16 : c1 // 16]),
            )

        def quantize_x(bf, c0, c1):
            cols = slice(c0, c1)
            nc.vector.quantize_mx(
                x_codes[:, cols].bitcast(E4M3), x_scales[:, cols], bf[:].rearrange("p s j -> p (s j)")
            )

        def dense_pass(c):
            cols = slice(c * P, (c + 1) * P)
            nc.tensor.matmul_mx(
                out=acc[c][:],
                lhsT=x_codes[:, cols].bitcast(E4M3),
                lhsT_scale=x_scales[:, cols],
                rhs=u_codes[:].bitcast(E4M3),
                rhs_scale=u_scales[:],
                start=False,
                stop=(c >= TILES // 2),
            )

        def table_pass(a, c):
            cols = slice(c * P, (c + 1) * P)
            nc.tensor.matmul_mx(
                out=acc[c][:],
                lhsT=picked_words[a][:, cols].bitcast(E4M3),
                lhsT_scale=picked[a][:, cols],
                rhs=w_codes[:, a, :].bitcast(E2M1),
                rhs_scale=w_scales[:, a, :],
                start=(a == 0),
                stop=(a == PASSES - 1 and c < TILES // 2),
            )

        nc.vector.tensor_copy(picked[0][:], scales01[:].bitcast(U8).indirect(offsets[:]))
        gather_words(0, 0, S)
        for quad in range(4):
            nc.sync.dma_start(
                picked[1][32 * quad : 32 * quad + 4, :].bitcast(I32),
                picked[0][32 * quad + 4 : 32 * quad + 8, :].bitcast(I32),
            )
        nc.vector.tensor_copy(picked[2][:], scales2[:].bitcast(U8).indirect(offsets[:]))
        gather_words(1, 0, S)
        for c in range(TILES):
            table_pass(0, c)
        quantize_x(x_bf[0], 0, HALF)
        nc.vector.quantize_mx(u_codes[:].bitcast(E4M3), u_scales[:], u_bf[:].rearrange("p n j -> p (n j)"))
        for c in range(TILES // 2):
            dense_pass(c)
        for c in range(TILES):
            table_pass(1, c)

        def finish(c, copy):
            result = keep.tile([P, M], F32, name="result%d" % c)
            copy(result[:], acc[c][:])
            nc.sync.dma_start(out[c * P : (c + 1) * P, :], result[:])

        gather_words(PASSES - 1, 0, HALF)
        for c in range(TILES // 2):
            table_pass(PASSES - 1, c)
            finish(c, nc.scalar.copy)
        gather_words(PASSES - 1, HALF, S)
        for c in range(TILES // 2, TILES):
            table_pass(PASSES - 1, c)
        nc.vector.tensor_copy(x_bf[2][:], x_raw[1][:, :, P:HALF].rearrange("p j s -> p s j"))
        for c, copy in ((2, nc.scalar.copy), (3, nc.vector.tensor_copy)):
            quantize_x(x_bf[c - 1], c * P, (c + 1) * P)
            dense_pass(c)
            finish(c, copy)
